import numpy as np
import ml_dtypes

BF16 = ml_dtypes.bfloat16


def bf(x):
    return np.asarray(x, np.float32).astype(BF16)


def f32(x):
    return np.asarray(x, np.float32)


def f64(x):
    return np.asarray(x).astype(np.float64)


def striped(idx):
    return np.tile(idx.reshape(-1, 16).T, (8, 1))


S, K, M, N, E, Q = 1024, 128, 256, 2048, 8, 256


def two_experts():
    first = np.random.permutation(S).reshape(E, S // E)
    return np.concatenate([np.random.permutation(np.concatenate([first[e], first[(e + 1) % E]])) for e in range(E)])


def setup_inputs():
    return {"table": bf(np.random.standard_normal((K, S))), "w": bf(np.random.standard_normal((E, K, M)) / np.sqrt(K)), "c": f32(0.2 + 0.8 * np.random.random_sample((1, N))), "offs": striped(two_experts())}


def reference(table, w, c, offs):
    idx = offs[:16].T.reshape(-1)
    x = f64(table)[:, idx]
    y = np.concatenate([f64(w)[e].T @ x[:, e * Q : (e + 1) * Q] for e in range(E)], axis=1)
    return y * f64(c)

@@ -1,0 +1,52 @@
+import concourse.mybir as mybir
+
+FLOPS = 2 * 128 * 256 * 2048
+
+BF16, F32, U16 = mybir.dt.bfloat16, mybir.dt.float32, mybir.dt.uint16
+MULT = mybir.AluOpType.mult
+
+K = 128
+S = 1024
+E = 8
+M = 256
+N = 2048
+Q = N // E
+LIST_COLS = Q // 16
+HALVES = M // 128
+
+
+def tile_gather_matmul_kernel(tc, table, w, c, offs, out):
+    nc = tc.nc
+    with (
+        tc.tile_pool(name="held", bufs=1) as held,
+        tc.tile_pool(name="staging", bufs=8) as staging,
+        tc.psum_pool(name="psum", bufs=8) as psum,
+    ):
+        offsets = held.tile([128, N // 16], U16, name="offsets")
+        tokens = held.tile([K, S], BF16, name="tokens")
+        weights = held.tile([K, E, M], BF16, name="weights")
+        c_rows = held.tile([128, N], F32, name="c_rows")
+
+        nc.sync.dma_start(offsets[:], offs)
+        nc.sync.dma_start(tokens[:], table)
+        nc.scalar.dma_start(weights[:], w.rearrange("e k m -> k e m"))
+        nc.scalar.dma_start(c_rows[:], c[0, :].partition_broadcast(128))
+
+        for pair in range(E // 2):
+            columns = slice(pair * 2 * Q, (pair + 1) * 2 * Q)
+            for half in range(HALVES):
+                rows = slice(half * 128, (half + 1) * 128)
+                bank = psum.tile([128, 2 * Q], F32, name="bank")
+                for side in range(2):
+                    e = 2 * pair + side
+                    piece = offsets[:, e * LIST_COLS : (e + 1) * LIST_COLS]
+                    nc.tensor.matmul(
+                        bank[:, side * Q : (side + 1) * Q],
+                        weights[:, e, rows],
+                        tokens[:].indirect(piece),
+                        start=True,
+                        stop=True,
+                    )
+                scaled = staging.tile([128, 2 * Q], F32, name="scaled")
+                nc.vector.tensor_tensor(scaled[:], bank[:], c_rows[:, columns], MULT)
+                nc.sync.dma_start(out[rows, columns], scaled[:])

@@ -1,4 +1,5 @@
 import concourse.mybir as mybir
+from concourse.masks import make_identity
 
 FLOPS = 2 * 128 * 256 * 2048
 
@@ -12,6 +13,8 @@ M = 256
 N = 2048
 Q = N // E
 LIST_COLS = Q // 16
+PAIRS = E // 2
+TURNS = 2 * Q // 128
 HALVES = M // 128
 
 
@@ -20,20 +23,32 @@ def tile_gather_matmul_kernel(tc, table, w, c, offs, out):
     with (
         tc.tile_pool(name="held", bufs=1) as held,
         tc.tile_pool(name="staging", bufs=8) as staging,
-        tc.psum_pool(name="psum", bufs=8) as psum,
+        tc.tile_pool(name="c_pool", bufs=PAIRS) as c_pool,
+        tc.psum_pool(name="c_psum", bufs=2) as c_psum,
+        tc.psum_pool(name="psum", bufs=6) as psum,
     ):
         offsets = held.tile([128, N // 16], U16, name="offsets")
         tokens = held.tile([K, S], BF16, name="tokens")
         weights = held.tile([K, E, M], BF16, name="weights")
-        c_rows = held.tile([128, N], F32, name="c_rows")
+        c_cols = held.tile([128, PAIRS, TURNS], F32, name="c_cols")
+        identity = held.tile([128, 128], F32, name="identity")
+        make_identity(nc, identity[:])
 
         nc.sync.dma_start(offsets[:], offs)
         nc.sync.dma_start(tokens[:], table)
+        nc.scalar.dma_start(c_cols[:], c[0, :].rearrange("(pair p i) -> p pair i", p=128, i=TURNS))
         nc.scalar.dma_start(weights[:], w.rearrange("e k m -> k e m"))
-        nc.scalar.dma_start(c_rows[:], c[0, :].partition_broadcast(128))
 
-        for pair in range(E // 2):
+        for pair in range(PAIRS):
             columns = slice(pair * 2 * Q, (pair + 1) * 2 * Q)
+
+            c_bank = c_psum.tile([128, TURNS, 128], F32, name="c_bank")
+            for i in range(TURNS):
+                repeated = c_cols[:, pair, i : i + 1].to_broadcast([128, 128])
+                nc.tensor.transpose(c_bank[:, i, :], repeated, identity[:])
+            c_rows = c_pool.tile([128, 128, TURNS], F32, name="c_rows")
+            nc.scalar.copy(c_rows[:], c_bank[:].rearrange("m i p -> m p i"))
+
             for half in range(HALVES):
                 rows = slice(half * 128, (half + 1) * 128)
                 bank = psum.tile([128, 2 * Q], F32, name="bank")
@@ -48,5 +63,5 @@ def tile_gather_matmul_kernel(tc, table, w, c, offs, out):
                         stop=True,
                     )
                 scaled = staging.tile([128, 2 * Q], F32, name="scaled")
-                nc.vector.tensor_tensor(scaled[:], bank[:], c_rows[:, columns], MULT)
+                nc.vector.tensor_tensor(scaled[:], bank[:], c_rows[:].rearrange("m p i -> m (p i)"), MULT)
                 nc.sync.dma_start(out[rows, columns], scaled[:])

@@ -14,8 +14,8 @@ N = 2048
 Q = N // E
 LIST_COLS = Q // 16
 PAIRS = E // 2
-TURNS = 2 * Q // 128
 HALVES = M // 128
+TURNS = 2 * Q // 128
 
 
 def tile_gather_matmul_kernel(tc, table, w, c, offs, out):
@@ -23,9 +23,7 @@ def tile_gather_matmul_kernel(tc, table, w, c, offs, out):
     with (
         tc.tile_pool(name="held", bufs=1) as held,
         tc.tile_pool(name="staging", bufs=8) as staging,
-        tc.tile_pool(name="c_pool", bufs=PAIRS) as c_pool,
-        tc.psum_pool(name="c_psum", bufs=2) as c_psum,
-        tc.psum_pool(name="psum", bufs=6) as psum,
+        tc.psum_pool(name="psum", bufs=8) as psum,
     ):
         offsets = held.tile([128, N // 16], U16, name="offsets")
         tokens = held.tile([K, S], BF16, name="tokens")
@@ -39,29 +37,31 @@ def tile_gather_matmul_kernel(tc, table, w, c, offs, out):
         nc.scalar.dma_start(c_cols[:], c[0, :].rearrange("(pair p i) -> p pair i", p=128, i=TURNS))
         nc.scalar.dma_start(weights[:], w.rearrange("e k m -> k e m"))
 
-        for pair in range(PAIRS):
-            columns = slice(pair * 2 * Q, (pair + 1) * 2 * Q)
+        banks = [[psum.tile([128, 2 * Q], F32, name="bank") for half in range(HALVES)] for pair in range(PAIRS)]
 
-            c_bank = c_psum.tile([128, TURNS, 128], F32, name="c_bank")
+        c_rows = [held.tile([128, 2 * Q], F32, name=f"c_rows{pair}") for pair in range(PAIRS)]
+        for pair in range(PAIRS):
+            blocks = banks[pair][0][:].rearrange("m (i p) -> m i p", i=TURNS)
             for i in range(TURNS):
                 repeated = c_cols[:, pair, i : i + 1].to_broadcast([128, 128])
-                nc.tensor.transpose(c_bank[:, i, :], repeated, identity[:])
-            c_rows = c_pool.tile([128, 128, TURNS], F32, name="c_rows")
-            nc.scalar.copy(c_rows[:], c_bank[:].rearrange("m i p -> m p i"))
+                nc.tensor.transpose(blocks[:, i, :], repeated, identity[:])
+            in_order = blocks.rearrange("m i p -> m p i")
+            nc.scalar.copy(c_rows[pair][:].rearrange("m (p i) -> m p i", i=TURNS), in_order)
 
+        for pair in range(PAIRS):
+            columns = slice(pair * 2 * Q, (pair + 1) * 2 * Q)
             for half in range(HALVES):
                 rows = slice(half * 128, (half + 1) * 128)
-                bank = psum.tile([128, 2 * Q], F32, name="bank")
                 for side in range(2):
                     e = 2 * pair + side
                     piece = offsets[:, e * LIST_COLS : (e + 1) * LIST_COLS]
                     nc.tensor.matmul(
-                        bank[:, side * Q : (side + 1) * Q],
+                        banks[pair][half][:, side * Q : (side + 1) * Q],
                         weights[:, e, rows],
                         tokens[:].indirect(piece),
                         start=True,
                         stop=True,
                     )
                 scaled = staging.tile([128, 2 * Q], F32, name="scaled")
-                nc.vector.tensor_tensor(scaled[:], bank[:], c_rows[:].rearrange("m p i -> m (p i)"), MULT)
+                nc.vector.tensor_tensor(scaled[:], banks[pair][half][:], c_rows[pair][:], MULT)
                 nc.sync.dma_start(out[rows, columns], scaled[:])

@@ -15,6 +15,7 @@ Q = N // E
 LIST_COLS = Q // 16
 PAIRS = E // 2
 HALVES = M // 128
+AHEAD = 2
 TURNS = 2 * Q // 128
 
 
@@ -27,7 +28,8 @@ def tile_gather_matmul_kernel(tc, table, w, c, offs, out):
     ):
         offsets = held.tile([128, N // 16], U16, name="offsets")
         tokens = held.tile([K, S], BF16, name="tokens")
-        weights = held.tile([K, E, M], BF16, name="weights")
+        weights_first = held.tile([K, 2, M], BF16, name="weights_first")
+        weights_rest = held.tile([K, E - 2, M], BF16, name="weights_rest")
         c_cols = held.tile([128, PAIRS, TURNS], F32, name="c_cols")
         identity = held.tile([128, 128], F32, name="identity")
         make_identity(nc, identity[:])
@@ -35,29 +37,35 @@ def tile_gather_matmul_kernel(tc, table, w, c, offs, out):
         nc.sync.dma_start(offsets[:], offs)
         nc.sync.dma_start(tokens[:], table)
         nc.scalar.dma_start(c_cols[:], c[0, :].rearrange("(pair p i) -> p pair i", p=128, i=TURNS))
-        nc.scalar.dma_start(weights[:], w.rearrange("e k m -> k e m"))
+        w_rows = w.rearrange("e k m -> k e m")
+        nc.scalar.dma_start(weights_first[:], w_rows[:, 0:2, :])
+        nc.scalar.dma_start(weights_rest[:], w_rows[:, 2:E, :])
 
         banks = [[psum.tile([128, 2 * Q], F32, name="bank") for half in range(HALVES)] for pair in range(PAIRS)]
-
+        last_banks = banks[PAIRS - 2] + banks[PAIRS - 1]
         c_rows = [held.tile([128, 2 * Q], F32, name=f"c_rows{pair}") for pair in range(PAIRS)]
-        for pair in range(PAIRS):
-            blocks = banks[pair][0][:].rearrange("m (i p) -> m i p", i=TURNS)
+
+        def spread(pair):
+            blocks = last_banks[pair][:].rearrange("m (i p) -> m i p", i=TURNS)
             for i in range(TURNS):
                 repeated = c_cols[:, pair, i : i + 1].to_broadcast([128, 128])
                 nc.tensor.transpose(blocks[:, i, :], repeated, identity[:])
             in_order = blocks.rearrange("m i p -> m p i")
             nc.scalar.copy(c_rows[pair][:].rearrange("m (p i) -> m p i", i=TURNS), in_order)
 
+        for pair in range(AHEAD):
+            spread(pair)
         for pair in range(PAIRS):
             columns = slice(pair * 2 * Q, (pair + 1) * 2 * Q)
             for half in range(HALVES):
                 rows = slice(half * 128, (half + 1) * 128)
                 for side in range(2):
                     e = 2 * pair + side
+                    expert_w = weights_first[:, e, rows] if e < 2 else weights_rest[:, e - 2, rows]
                     piece = offsets[:, e * LIST_COLS : (e + 1) * LIST_COLS]
                     nc.tensor.matmul(
                         banks[pair][half][:, side * Q : (side + 1) * Q],
-                        weights[:, e, rows],
+                        expert_w,
                         tokens[:].indirect(piece),
                         start=True,
                         stop=True,
@@ -65,3 +73,5 @@ def tile_gather_matmul_kernel(tc, table, w, c, offs, out):
                 scaled = staging.tile([128, 2 * Q], F32, name="scaled")
                 nc.vector.tensor_tensor(scaled[:], banks[pair][half][:], c_rows[pair][:], MULT)
                 nc.sync.dma_start(out[rows, columns], scaled[:])
+            if pair + AHEAD < PAIRS:
+                spread(pair + AHEAD)

import concourse.mybir as mybir
from concourse.masks import make_identity

FLOPS = 2 * 128 * 256 * 2048

BF16, F32, U16 = mybir.dt.bfloat16, mybir.dt.float32, mybir.dt.uint16
MULT = mybir.AluOpType.mult

K = 128
S = 1024
E = 8
M = 256
N = 2048
Q = N // E
LIST_COLS = Q // 16
PAIRS = E // 2
HALVES = M // 128
AHEAD = 2
TURNS = 2 * Q // 128


def tile_gather_matmul_kernel(tc, table, w, c, offs, out):
    nc = tc.nc
    with (
        tc.tile_pool(name="held", bufs=1) as held,
        tc.tile_pool(name="staging", bufs=8) as staging,
        tc.psum_pool(name="psum", bufs=8) as psum,
    ):
        offsets = held.tile([128, N // 16], U16, name="offsets")
        tokens = held.tile([K, S], BF16, name="tokens")
        weights_first = held.tile([K, 2, M], BF16, name="weights_first")
        weights_rest = held.tile([K, E - 2, M], BF16, name="weights_rest")
        c_cols = held.tile([128, PAIRS, TURNS], F32, name="c_cols")
        identity = held.tile([128, 128], F32, name="identity")
        make_identity(nc, identity[:])

        nc.sync.dma_start(offsets[:], offs)
        nc.sync.dma_start(tokens[:], table)
        nc.scalar.dma_start(c_cols[:], c[0, :].rearrange("(pair p i) -> p pair i", p=128, i=TURNS))
        w_rows = w.rearrange("e k m -> k e m")
        nc.scalar.dma_start(weights_first[:], w_rows[:, 0:2, :])
        nc.scalar.dma_start(weights_rest[:], w_rows[:, 2:E, :])

        banks = [[psum.tile([128, 2 * Q], F32, name="bank") for half in range(HALVES)] for pair in range(PAIRS)]
        last_banks = banks[PAIRS - 2] + banks[PAIRS - 1]
        c_rows = [held.tile([128, 2 * Q], F32, name=f"c_rows{pair}") for pair in range(PAIRS)]

        def spread(pair):
            blocks = last_banks[pair][:].rearrange("m (i p) -> m i p", i=TURNS)
            for i in range(TURNS):
                repeated = c_cols[:, pair, i : i + 1].to_broadcast([128, 128])
                nc.tensor.transpose(blocks[:, i, :], repeated, identity[:])
            in_order = blocks.rearrange("m i p -> m p i")
            nc.scalar.copy(c_rows[pair][:].rearrange("m (p i) -> m p i", i=TURNS), in_order)

        for pair in range(AHEAD):
            spread(pair)
        for pair in range(PAIRS):
            columns = slice(pair * 2 * Q, (pair + 1) * 2 * Q)
            for half in range(HALVES):
                rows = slice(half * 128, (half + 1) * 128)
                for side in range(2):
                    e = 2 * pair + side
                    expert_w = weights_first[:, e, rows] if e < 2 else weights_rest[:, e - 2, rows]
                    piece = offsets[:, e * LIST_COLS : (e + 1) * LIST_COLS]
                    nc.tensor.matmul(
                        banks[pair][half][:, side * Q : (side + 1) * Q],
                        expert_w,
                        tokens[:].indirect(piece),
                        start=True,
                        stop=True,
                    )
                scaled = staging.tile([128, 2 * Q], F32, name="scaled")
                nc.vector.tensor_tensor(scaled[:], banks[pair][half][:], c_rows[pair][:], MULT)
                nc.sync.dma_start(out[rows, columns], scaled[:])
            if pair + AHEAD < PAIRS:
                spread(pair + AHEAD)
